import numpy as np
import ml_dtypes


def mxq(x, axis, fmt="e4m3"):
    dtype, down = {"e4m3": (ml_dtypes.float8_e4m3fn, 7), "e5m2": (ml_dtypes.float8_e5m2, 14)}[fmt]
    v = np.moveaxis(np.asarray(x, np.float32).astype(ml_dtypes.bfloat16).astype(np.float64), axis, -1)
    blocks = v.reshape(v.shape[:-1] + (-1, 32))
    amax = np.abs(blocks).max(-1, keepdims=True)
    byte = np.maximum(np.where(amax > 0, np.frexp(amax)[1] - 1 + 127, 0) - down, 1)
    scale = np.exp2(byte - 127.0)
    codes = (blocks / scale).astype(np.float32).astype(dtype).astype(np.float64)
    return np.moveaxis((codes * scale).reshape(v.shape), -1, axis)


WIDE = False


def mx_kscale(k):
    if not WIDE:
        return np.ones(k)
    levels = np.array([10, -10, 5, -5, 0])
    if k % 512:
        return np.exp2(np.random.permutation(np.resize(levels, k // 32))).repeat(32)
    a = np.empty((k // 512, 16))
    for p in range(k // 512):
        a[p, :8] = np.random.permutation(np.resize(levels, 8))
        for g in range(8):
            far = levels[np.abs(levels - a[p, g]) >= 10]
            a[p, g + 8] = far[np.random.randint(len(far))]
    return np.exp2(a.ravel()).repeat(32)


def f64(x):
    return np.asarray(x).astype(np.float64)


def striped(idx):
    return np.tile(idx.reshape(-1, 16).T, (8, 1)).astype(np.uint16)


def unstriped(offs):
    return offs[:16].T.reshape(-1).astype(np.int64)


def striped8(idx):
    return np.concatenate([x.reshape(-1, 16).T for x in idx]).astype(np.uint16)


def runs(offs, k):
    lists = np.stack([offs[16 * r : 16 * r + 16].T.reshape(-1) for r in range(8)]).astype(np.int64)
    return lists[np.arange(k) % 512 // 64]


def pack_weight(w):
    k, n = w.shape
    w = f64(np.asarray(w, np.float32).astype(ml_dtypes.bfloat16)).reshape(k // 32, 32, n)
    amax = np.abs(w).max(1)
    byte = np.clip(np.where(amax > 0, np.frexp(amax)[1] - 1 + 127 - 7, 1), 1, 254)
    scaled = (w * np.exp2(127.0 - byte)[:, None, :]).reshape(k, n).astype(np.float32)
    words = np.ascontiguousarray(scaled.reshape(k // 512, 128, 4, n).transpose(0, 1, 3, 2)).astype(ml_dtypes.float8_e4m3fn).view(np.uint8)
    return words, np.ascontiguousarray(byte.astype(np.uint8).reshape(k // 512, 16, n))


def unpack_weight(words, scales):
    g, p, n, _ = words.shape
    vals = np.ascontiguousarray(words).view(ml_dtypes.float8_e4m3fn).astype(np.float64) * np.repeat(np.exp2(scales.astype(np.float64) - 127.0), 8, axis=1)[..., None]
    return vals.transpose(0, 1, 3, 2).reshape(g * 512, n)

def planes(y):
    n, m = y.shape
    v = y.astype(np.float32).astype(ml_dtypes.bfloat16).astype(np.float64).reshape(n // 32, 32, m)
    top = np.abs(v).max(1)
    byte = np.clip(np.where(top > 0, np.frexp(top)[1] - 1 + 127 - 7, 1), 1, 254)
    codes = (v * np.exp2(127.0 - byte)[:, None, :]).reshape(n, m).astype(np.float32).astype(ml_dtypes.float8_e4m3fn).view(np.uint8)
    words = codes.reshape(n // 512, 128, 4, m).transpose(0, 1, 3, 2)
    return np.ascontiguousarray(words), np.ascontiguousarray(byte.astype(np.uint8).reshape(n // 512, 16, m))


K, T, S, N, H, W = 512, 2048, 512, 512, 512, 256


def setup_inputs():
    n = np.random.standard_normal
    s = mx_kscale(K)[:, None]
    u = mx_kscale(H)
    packed_xT = pack_weight(n((K, T)) * s)
    packed_w1 = pack_weight(n((K, H)) / np.sqrt(K) / s)
    packed_w2 = pack_weight(n((H, N)) / np.sqrt(H) / u[:, None])
    packed_w3 = pack_weight(n((K, N)) / np.sqrt(K) / s)
    perm = np.stack([np.random.permutation(S) for _ in range(8)])
    return {
        "x_words": packed_xT[0],
        "x_scales": packed_xT[1],
        "w1_words": packed_w1[0],
        "w1_scales": packed_w1[1],
        "gn": (np.random.uniform(0.5, 1.5, (H, 1)) * u[:, None]).astype(np.float32),
        "w2_words": packed_w2[0],
        "w2_scales": packed_w2[1],
        "w3_words": packed_w3[0],
        "w3_scales": packed_w3[1],
        "offs": striped(np.random.permutation(T)[:S]),
        "n1": striped8(perm[:, :W]),
        "n2": striped8(perm[:, W:]),
        "n3": striped8(np.stack([np.random.permutation(S) for _ in range(8)])),
        "two": striped(np.random.permutation(T)[:S]),
        "n4": striped(np.random.permutation(S)),
        "n5": striped(np.random.permutation(S)),
    }


def reference(x_words, x_scales, w1_words, w1_scales, gn, w2_words, w2_scales, w3_words, w3_scales, offs, n1, n2, n3, two, n4, n5):
    xq = unpack_weight(x_words, x_scales)[:, unstriped(offs)]
    y = unpack_weight(w1_words, w1_scales).T @ xq
    pa = y[np.arange(H)[:, None], runs(n1, H)]
    pb = y[np.arange(H)[:, None], runs(n2, H)]
    ra = pa - (0.5 * pb)
    ds = y.copy()
    ds[np.arange(H)[:, None], runs(n2, H)] = ra
    z = f64(gn) * (ds - (0.5 * (ds[np.arange(H)[:, None], runs(n3, H)])))
    h = unpack_weight(w2_words, w2_scales).T @ mxq(z, 0, "e4m3")
    x_two = unpack_weight(x_words, x_scales)[:, unstriped(two)]
    d = unpack_weight(w3_words, w3_scales).T @ x_two
    out_0 = h[:, unstriped(n4)] - (np.tanh(d) * d[:, unstriped(n5)])
    return (out_0,) + planes(out_0)

@@ -1,0 +1,325 @@
+from contextlib import ExitStack
+
+import concourse.mybir as mybir
+
+K, T, S, N, H, W = 512, 2048, 512, 512, 512, 256
+FLOPS = 3 * 2 * 512 * 512 * 512
+
+F32 = mybir.dt.float32
+BF16 = mybir.dt.bfloat16
+I32 = mybir.dt.int32
+U32 = mybir.dt.uint32
+U16 = mybir.dt.uint16
+U8 = mybir.dt.uint8
+FP8X4 = mybir.dt.float8_e4m3fn_x4
+MULT = mybir.AluOpType.mult
+ADD = mybir.AluOpType.add
+SUB = mybir.AluOpType.subtract
+COPY = mybir.ActivationFunctionType.Copy
+TANH = mybir.ActivationFunctionType.Tanh
+
+P = 128
+PACK = 4
+HALF = S // 2
+
+
+def tile_picked_latesoftbfoldd_none_po_kernel(
+    tc, x_words, x_scales, w1_words, w1_scales, gn, w2_words, w2_scales, w3_words, w3_scales,
+    offs, n1, n2, n3, two, n4, n5, out_0, out_1, out_2,
+):
+    nc = tc.nc
+    with ExitStack() as ctx:
+        lists = ctx.enter_context(tc.tile_pool(name="lists", bufs=1))
+        keep = ctx.enter_context(tc.tile_pool(name="keep", bufs=1))
+        psum = ctx.enter_context(tc.psum_pool(name="psum", bufs=1))
+
+        def load_list(src, name):
+            tile = lists.tile(list(src.shape), U16, name=name)
+            nc.sync.dma_start(tile[:], src)
+            return tile
+
+        def load_words(src, cols, name, queue):
+            tile = keep.tile([P, cols], I32, name=name, align_bytes=64)
+            queue.dma_start(tile[:], src[0].rearrange("p c r -> p (c r)").bitcast(I32))
+            return tile
+
+        def load_scale_rows(tile, src, first, queue):
+            for q in range(4):
+                queue.dma_start(
+                    tile[32 * q + first : 32 * q + first + 4, :].bitcast(I32),
+                    src[0, 4 * q : 4 * q + 4, :].bitcast(I32),
+                )
+
+        def load_scale_rows_repeated(tile, src, queue):
+            for q in range(4):
+                queue.dma_start(
+                    tile[32 * q : 32 * q + 32, :].bitcast(I32),
+                    src[0, 4 * q : 4 * q + 4, :].bitcast(I32).partition_broadcast(8),
+                )
+
+        def deal(src, dtype, name):
+            tile = keep.tile([P, 512], dtype, name=name, align_bytes=64)
+            nc.vector.tensor_copy(
+                tile[:].rearrange("p (t m) -> p m t", t=PACK),
+                src[:].rearrange("p (m t) -> p m t", t=PACK),
+            )
+            return tile
+
+        def half_list(tile, a):
+            return tile[:, a * (HALF // 16) : (a + 1) * (HALF // 16)]
+
+        def cols(a):
+            return slice(a * HALF, (a + 1) * HALF)
+
+        xs = keep.tile([P, T], U8, name="xs", align_bytes=64)
+        w1s = keep.tile([P, H], U8, name="w1s", align_bytes=64)
+        w23s = keep.tile([P, N], U8, name="w23s", align_bytes=64)
+        nc.gpsimd.memset(w23s[:].bitcast(I32), 0)
+
+        offs_t = load_list(offs, "offs_t")
+        load_scale_rows_repeated(xs, x_scales, nc.sync)
+        two_t = load_list(two, "two_t")
+        w1w = load_words(w1_words, H, "w1w", nc.sync)
+        xw = load_words(x_words, T, "xw", nc.sync)
+        load_scale_rows_repeated(w1s, w1_scales, nc.sync)
+        gain = keep.tile([P, PACK], F32, name="gain")
+        nc.sync.dma_start(gain[:], gn.rearrange("(p t) o -> p (t o)", t=PACK))
+        n1_t = load_list(n1, "n1_t")
+        n2_t = load_list(n2, "n2_t")
+        w3w = load_words(w3_words, N, "w3w", nc.sync)
+        n3_t = load_list(n3, "n3_t")
+        load_scale_rows(w23s, w3_scales, 0, nc.sync)
+        load_scale_rows(w23s, w2_scales, 4, nc.sync)
+        n5_t = load_list(n5, "n5_t")
+        w2w = load_words(w2_words, N, "w2w", nc.sync)
+        n4_t = load_list(n4, "n4_t")
+
+        def pick_scales(lst, name):
+            tile = keep.tile([P, S], U8, name=name, align_bytes=64)
+            nc.vector.tensor_copy(tile[:], xs[:].indirect(lst[:]))
+            return tile
+
+        def pick_words(lst, name):
+            tile = keep.tile([P, S], I32, name=name, align_bytes=64)
+            nc.vector.tensor_copy(tile[:].bitcast(U32), xw[:].bitcast(U32).indirect(lst[:]))
+            return tile
+
+        def product(bank, ww, ws, first, t, codes, scales):
+            m = slice(P * t, P * (t + 1))
+            nc.tensor.matmul_mx(
+                out=bank, lhsT=ww[:, m].bitcast(FP8X4), lhsT_scale=ws[first:P, m],
+                rhs=codes.bitcast(FP8X4), rhs_scale=scales, start=True, stop=True,
+            )
+
+        xa_s = pick_scales(offs_t, "xa_s")
+        xb_s = pick_scales(two_t, "xb_s")
+        w1w_d = deal(w1w, I32, "w1w_d")
+        xa_w = pick_words(offs_t, "xa_w")
+        w1s_d = deal(w1s, U8, "w1s_d")
+        y_ps = [psum.tile([P, S], F32, name="y_ps%d" % t, tag="yh%d" % t) for t in range(PACK)]
+        for t in range(PACK):
+            product(y_ps[t][:], w1w_d, w1s_d, 0, t, xa_w[:], xa_s[:])
+        xb_w = pick_words(two_t, "xb_w")
+
+        ds = [keep.tile([P, 2 * S], F32, name="ds%d" % t) for t in range(PACK)]
+        d_sb = [keep.tile([P, S + 16], F32, name="d_sb%d" % t) for t in range(PACK)]
+        for t in range(PACK):
+            nc.gpsimd.memset(ds[t][:, S:], 0.0)
+        for t in range(PACK):
+            nc.gpsimd.memset(d_sb[t][:, S:], 0.0)
+        pa = [keep.tile([P, W], F32, name="pa%d" % t) for t in range(PACK)]
+        pb = [keep.tile([P, W], F32, name="pb%d" % t) for t in range(PACK)]
+        far = [keep.tile([P, S], F32, name="far%d" % t) for t in range(PACK)]
+        z_rows = keep.tile([P, PACK, S], BF16, name="z_rows")
+        th = [keep.tile([P, S], F32, name="th%d" % t, tag="th%d" % t) for t in range(PACK)]
+        d5 = [keep.tile([P, S], F32, name="d5%d" % t, tag="d5%d" % t) for t in range(PACK)]
+        gate = {}
+        h_sb = [keep.tile([P, S], F32, name="h_sb%d" % t) for t in range(PACK)]
+        d_ps = [psum.tile([P, S], F32, name="d_ps%d" % t, tag="d%d" % t) for t in range(PACK)]
+        h_ps = [psum.tile([P, S], F32, name="h_ps%d" % t, tag="yh%d" % t) for t in range(PACK)]
+
+        def part_list(tile, c):
+            return tile[:, c.start // 16 : c.stop // 16]
+
+        def y_out(t):
+            nc.scalar.activation(ds[t][:, :S], y_ps[t][:], COPY, scale=gain[:, t : t + 1])
+
+        def fetch_a(t):
+            nc.scalar.activation(pa[t][:], ds[t][:].indirect(n1_t[:]), COPY)
+
+        def fetch_b(t):
+            nc.vector.tensor_scalar(pb[t][:], ds[t][:].indirect(n2_t[:]), -0.5, 0.0, MULT, ADD)
+
+        def put(t):
+            nc.vector.tensor_tensor(ds[t][:].indirect(n2_t[:]), pa[t][:], pb[t][:], ADD)
+
+        def fetch_far(t, c):
+            nc.scalar.activation(far[t][:, c], ds[t][:].indirect(part_list(n3_t, c)), COPY)
+
+        def z_row(t, c):
+            nc.vector.scalar_tensor_tensor(z_rows[:, t, c], far[t][:, c], -0.5, ds[t][:, c], MULT, ADD)
+
+        def d_out(t):
+            nc.scalar.activation(d_sb[t][:, :S], d_ps[t][:], COPY)
+
+        def d_out_v(t):
+            nc.vector.tensor_copy(d_sb[t][:, :S], d_ps[t][:])
+
+        def d_tanh(t):
+            nc.scalar.activation(th[t][:], d_ps[t][:], TANH)
+
+        def d_fetch(t):
+            nc.scalar.activation(d5[t][:], d_sb[t][:].indirect(n5_t[:]), COPY)
+
+        def d_gate(t):
+            nc.vector.tensor_tensor(gate[t // 2][:, t % 2, :], th[t][:], d5[t][:], MULT)
+
+        def group(rows, width, name):
+            grouped = keep.tile([P, width, PACK], BF16, name=name + "_g", align_bytes=64)
+            nc.vector.tensor_copy(
+                grouped[:].rearrange("p (c i) t -> p c t i", i=4),
+                rows.rearrange("p t (c i) -> p c t i", i=4),
+            )
+            return grouped
+
+        def z_codes(grouped, name):
+            z_w = keep.tile([P, HALF], I32, name=name + "_w", tag=name + "_w", align_bytes=64)
+            z_s = keep.tile([P, HALF], U8, name=name + "_s", align_bytes=64)
+            nc.vector.quantize_mx(
+                out=z_w[:].bitcast(FP8X4), scales=z_s[:], in_=grouped[:].rearrange("p j t -> p (j t)")
+            )
+            return z_w, z_s
+
+        def z_products(codes):
+            for t in range(PACK):
+                for a in range(2):
+                    product(h_ps[t][:, cols(a)], w2w_d, w23s_d, 4, t, codes[a][0][:], codes[a][1][:])
+
+        def h_out(t, c):
+            nc.vector.tensor_copy(h_sb[t][:, c], h_ps[t][:, c])
+
+        def h_out_s(t, c):
+            nc.scalar.activation(h_sb[t][:, c], h_ps[t][:, c], COPY)
+
+        out_rows = out_0.rearrange("(p t) j -> p t j", t=PACK)
+        out_words = out_1[0].rearrange("p c r -> p (c r)").bitcast(I32)
+        o_s = keep.tile([P, S], U8, name="o_s", align_bytes=64)
+        parts = [slice(0, 256), slice(256, 384), slice(384, S)]
+        h4 = {}
+        res = [keep.tile([P, PACK, c.stop - c.start], F32, name="res_%d" % c.start) for c in parts]
+
+        def h_room(a, tag):
+            h4[a] = keep.tile([P, PACK, parts[a].stop - parts[a].start], F32, name="h4_%d" % a, tag=tag)
+
+        def h_fetch(t, a):
+            nc.scalar.activation(h4[a][:, t, :], h_sb[t][:].indirect(part_list(n4_t, parts[a])), COPY)
+
+        def result(u, a):
+            ts = slice(2 * u, 2 * u + 2)
+            nc.vector.tensor_tensor(res[a][:, ts, :], h4[a][:, ts, :], gate[u][:, :, parts[a]], SUB)
+
+        def store_result(a):
+            nc.sync.dma_start(out_rows[:, :, parts[a]], res[a][:])
+
+        def planes(grouped, a):
+            c = parts[a]
+            o_w = keep.tile([P, c.stop - c.start], I32, name="o_w%d" % a, align_bytes=64)
+            nc.vector.quantize_mx(
+                out=o_w[:].bitcast(FP8X4), scales=o_s[:, c], in_=grouped[:].rearrange("p j t -> p (j t)")
+            )
+            nc.sync.dma_start(out_words[:, c], o_w[:])
+
+        def store_scales():
+            for q in range(4):
+                queue = nc.sync if q % 2 == 0 else nc.scalar
+                queue.dma_start(out_2[0, 4 * q : 4 * q + 4, :].bitcast(I32), o_s[32 * q : 32 * q + 4, :].bitcast(I32))
+
+        whole = slice(0, S)
+        y_out(0)
+        fetch_a(0)
+        fetch_b(0)
+        put(0)
+        y_out(1)
+        fetch_a(1)
+        fetch_b(1)
+        put(1)
+        y_out(2)
+        fetch_a(2)
+        fetch_far(0, whole)
+        w23s_d = deal(w23s, U8, "w23s_d")
+        w3w_d = deal(w3w, I32, "w3w_d")
+        for t in range(PACK): product(d_ps[t][:], w3w_d, w23s_d, 0, t, xb_w[:], xb_s[:])
+        fetch_b(2)
+        put(2)
+        y_out(3)
+        fetch_a(3)
+        fetch_far(1, whole)
+        z_row(0, whole)
+        fetch_b(3)
+        put(3)
+        d_out(0)
+        d_tanh(0)
+        d_fetch(0)
+        fetch_far(2, whole)
+        z_row(1, whole)
+        d_out(1)
+        d_tanh(1)
+        z_row(2, whole)
+        w2w_d = deal(w2w, I32, "w2w_d")
+        fetch_far(3, cols(0))
+        fetch_far(3, cols(1))
+        gate[0] = keep.tile([P, 2, S], F32, name="gate0")
+        z_row(3, cols(0))
+        z_row(3, cols(1))
+        g0 = group(z_rows[:, :, cols(0)], HALF, "z0")
+        g1 = group(z_rows[:, :, cols(1)], HALF, "z1")
+        c0 = z_codes(g0, "z0")
+        c1 = z_codes(g1, "z1")
+        z_products([c0, c1])
+        d_gate(0)
+        d_fetch(1)
+        d_gate(1)
+        d_out(2)
+        d_tanh(2)
+        d_fetch(2)
+        d_out(3)
+        d_tanh(3)
+        d_fetch(3)
+        gate[1] = keep.tile([P, 2, S], F32, name="gate1", tag="z1_w", align_bytes=64)
+        h_out(0, whole)
+        h_out(1, whole)
+        h_out(2, whole)
+        d_gate(2)
+        h_out(3, whole)
+        d_gate(3)
+        h_room(0, "h4_0")
+        h_room(1, "th3")
+        h_room(2, "d53")
+        h_fetch(0, 0)
+        h_fetch(1, 0)
+        result(0, 0)
+        h_fetch(2, 0)
+        h_fetch(3, 0)
+        result(1, 0)
+        store_result(0)
+        h_fetch(0, 1)
+        h_fetch(1, 1)
+        result(0, 1)
+        h_fetch(2, 1)
+        h_fetch(3, 1)
+        o0 = group(res[0][:], 256, "o0")
+        result(1, 1)
+        store_result(1)
+        planes(o0, 0)
+        h_fetch(0, 2)
+        h_fetch(1, 2)
+        o1 = group(res[1][:], 128, "o1")
+        result(0, 2)
+        h_fetch(2, 2)
+        h_fetch(3, 2)
+        planes(o1, 1)
+        result(1, 2)
+        store_result(2)
+        o2 = group(res[2][:], 128, "o2")
+        planes(o2, 2)
+        store_scales()

@@ -50,9 +50,9 @@ def tile_picked_latesoftbfoldd_none_po_kernel(
                     src[0, 4 * q : 4 * q + 4, :].bitcast(I32),
                 )
 
-        def load_scale_rows_repeated(tile, src, queue):
+        def load_scale_rows_repeated(tile, src, queues):
             for q in range(4):
-                queue.dma_start(
+                queues[q].dma_start(
                     tile[32 * q : 32 * q + 32, :].bitcast(I32),
                     src[0, 4 * q : 4 * q + 4, :].bitcast(I32).partition_broadcast(8),
                 )
@@ -72,25 +72,25 @@ def tile_picked_latesoftbfoldd_none_po_kernel(
             return slice(a * HALF, (a + 1) * HALF)
 
         xs = keep.tile([P, T], U8, name="xs", align_bytes=64)
-        w1s = keep.tile([P, H], U8, name="w1s", align_bytes=64)
-        w23s = keep.tile([P, N], U8, name="w23s", align_bytes=64)
-        nc.gpsimd.memset(w23s[:].bitcast(I32), 0)
+        w1s = keep.tile([P, H], U8, name="w1s", tag="w1s", align_bytes=64)
+        w2s = keep.tile([P, N], U8, name="w2s", align_bytes=64)
+        w3s = keep.tile([P, N], U8, name="w3s", tag="w3s", align_bytes=64)
 
         offs_t = load_list(offs, "offs_t")
-        load_scale_rows_repeated(xs, x_scales, nc.sync)
+        load_scale_rows_repeated(xs, x_scales, [nc.scalar, nc.scalar, nc.scalar, nc.sync])
         two_t = load_list(two, "two_t")
         w1w = load_words(w1_words, H, "w1w", nc.sync)
-        xw = load_words(x_words, T, "xw", nc.sync)
-        load_scale_rows_repeated(w1s, w1_scales, nc.sync)
+        xw = load_words(x_words, T, "xw", nc.scalar)
+        load_scale_rows_repeated(w1s, w1_scales, [nc.sync] * 4)
         gain = keep.tile([P, PACK], F32, name="gain")
-        nc.sync.dma_start(gain[:], gn.rearrange("(p t) o -> p (t o)", t=PACK))
+        nc.scalar.dma_start(gain[:], gn.rearrange("(p t) o -> p (t o)", t=PACK))
         n1_t = load_list(n1, "n1_t")
         n2_t = load_list(n2, "n2_t")
-        w3w = load_words(w3_words, N, "w3w", nc.sync)
+        w3w = load_words(w3_words, N, "w3w", nc.scalar)
+        load_scale_rows_repeated(w3s, w3_scales, [nc.scalar, nc.scalar, nc.scalar, nc.sync])
         n3_t = load_list(n3, "n3_t")
-        load_scale_rows(w23s, w3_scales, 0, nc.sync)
-        load_scale_rows(w23s, w2_scales, 4, nc.sync)
         n5_t = load_list(n5, "n5_t")
+        load_scale_rows_repeated(w2s, w2_scales, [nc.sync] * 4)
         w2w = load_words(w2_words, N, "w2w", nc.sync)
         n4_t = load_list(n4, "n4_t")
 
@@ -99,8 +99,8 @@ def tile_picked_latesoftbfoldd_none_po_kernel(
             nc.vector.tensor_copy(tile[:], xs[:].indirect(lst[:]))
             return tile
 
-        def pick_words(lst, name):
-            tile = keep.tile([P, S], I32, name=name, align_bytes=64)
+        def pick_words(lst, name, tag):
+            tile = keep.tile([P, S], I32, name=name, tag=tag, align_bytes=64)
             nc.vector.tensor_copy(tile[:].bitcast(U32), xw[:].bitcast(U32).indirect(lst[:]))
             return tile
 
@@ -114,12 +114,12 @@ def tile_picked_latesoftbfoldd_none_po_kernel(
         xa_s = pick_scales(offs_t, "xa_s")
         xb_s = pick_scales(two_t, "xb_s")
         w1w_d = deal(w1w, I32, "w1w_d")
-        xa_w = pick_words(offs_t, "xa_w")
+        xa_w = pick_words(offs_t, "xa_w", "xa_w")
         w1s_d = deal(w1s, U8, "w1s_d")
         y_ps = [psum.tile([P, S], F32, name="y_ps%d" % t, tag="yh%d" % t) for t in range(PACK)]
         for t in range(PACK):
             product(y_ps[t][:], w1w_d, w1s_d, 0, t, xa_w[:], xa_s[:])
-        xb_w = pick_words(two_t, "xb_w")
+        xb_w = pick_words(two_t, "xb_w", "w1s")
 
         ds = [keep.tile([P, 2 * S], F32, name="ds%d" % t) for t in range(PACK)]
         d_sb = [keep.tile([P, S + 16], F32, name="d_sb%d" % t) for t in range(PACK)]
@@ -128,7 +128,7 @@ def tile_picked_latesoftbfoldd_none_po_kernel(
         for t in range(PACK):
             nc.gpsimd.memset(d_sb[t][:, S:], 0.0)
         pa = [keep.tile([P, W], F32, name="pa%d" % t) for t in range(PACK)]
-        pb = [keep.tile([P, W], F32, name="pb%d" % t) for t in range(PACK)]
+        pb = {}
         far = [keep.tile([P, S], F32, name="far%d" % t) for t in range(PACK)]
         z_rows = keep.tile([P, PACK, S], BF16, name="z_rows")
         th = [keep.tile([P, S], F32, name="th%d" % t, tag="th%d" % t) for t in range(PACK)]
@@ -148,6 +148,7 @@ def tile_picked_latesoftbfoldd_none_po_kernel(
             nc.scalar.activation(pa[t][:], ds[t][:].indirect(n1_t[:]), COPY)
 
         def fetch_b(t):
+            pb[t] = keep.tile([P, W], F32, name="pb%d" % t, tag="pb%d" % t)
             nc.vector.tensor_scalar(pb[t][:], ds[t][:].indirect(n2_t[:]), -0.5, 0.0, MULT, ADD)
 
         def put(t):
@@ -175,7 +176,7 @@ def tile_picked_latesoftbfoldd_none_po_kernel(
             nc.vector.tensor_tensor(gate[t // 2][:, t % 2, :], th[t][:], d5[t][:], MULT)
 
         def group(rows, width, name):
-            grouped = keep.tile([P, width, PACK], BF16, name=name + "_g", align_bytes=64)
+            grouped = keep.tile([P, width, PACK], BF16, name=name + "_g", tag=name + "_g", align_bytes=64)
             nc.vector.tensor_copy(
                 grouped[:].rearrange("p (c i) t -> p c t i", i=4),
                 rows.rearrange("p t (c i) -> p c t i", i=4),
@@ -193,7 +194,7 @@ def tile_picked_latesoftbfoldd_none_po_kernel(
         def z_products(codes):
             for t in range(PACK):
                 for a in range(2):
-                    product(h_ps[t][:, cols(a)], w2w_d, w23s_d, 4, t, codes[a][0][:], codes[a][1][:])
+                    product(h_ps[t][:, cols(a)], w2w_d, w2s_d, 0, t, codes[a][0][:], codes[a][1][:])
 
         def h_out(t, c):
             nc.vector.tensor_copy(h_sb[t][:, c], h_ps[t][:, c])
@@ -204,19 +205,22 @@ def tile_picked_latesoftbfoldd_none_po_kernel(
         out_rows = out_0.rearrange("(p t) j -> p t j", t=PACK)
         out_words = out_1[0].rearrange("p c r -> p (c r)").bitcast(I32)
         o_s = keep.tile([P, S], U8, name="o_s", align_bytes=64)
-        parts = [slice(0, 256), slice(256, 384), slice(384, S)]
+        parts = [slice(0, HALF), slice(HALF, S)]
         h4 = {}
         res = [keep.tile([P, PACK, c.stop - c.start], F32, name="res_%d" % c.start) for c in parts]
 
-        def h_room(a, tag):
-            h4[a] = keep.tile([P, PACK, parts[a].stop - parts[a].start], F32, name="h4_%d" % a, tag=tag)
+        def h_room(u, a):
+            h4[u, a] = keep.tile([P, 2, parts[a].stop - parts[a].start], F32, name="h4_%d_%d" % (u, a), tag="h4_%d" % u)
 
         def h_fetch(t, a):
-            nc.scalar.activation(h4[a][:, t, :], h_sb[t][:].indirect(part_list(n4_t, parts[a])), COPY)
+            nc.scalar.activation(h4[t // 2, a][:, t % 2, :], h_sb[t][:].indirect(part_list(n4_t, parts[a])), COPY)
 
         def result(u, a):
             ts = slice(2 * u, 2 * u + 2)
-            nc.vector.tensor_tensor(res[a][:, ts, :], h4[a][:, ts, :], gate[u][:, :, parts[a]], SUB)
+            nc.vector.tensor_tensor(res[a][:, ts, :], h4[u, a][:], gate[u][:, :, parts[a]], SUB)
+
+        def result_row(t, a):
+            nc.vector.tensor_tensor(res[a][:, t, :], h4[t // 2, a][:, t % 2, :], gate[t // 2][:, t % 2, parts[a]], SUB)
 
         def store_result(a):
             nc.sync.dma_start(out_rows[:, :, parts[a]], res[a][:])
@@ -239,20 +243,20 @@ def tile_picked_latesoftbfoldd_none_po_kernel(
         fetch_a(0)
         fetch_b(0)
         put(0)
+        w3s_d = deal(w3s, U8, "w3s_d")
+        w3w_d = deal(w3w, I32, "w3w_d")
+        for t in range(PACK): product(d_ps[t][:], w3w_d, w3s_d, 0, t, xb_w[:], xb_s[:])
         y_out(1)
         fetch_a(1)
         fetch_b(1)
         put(1)
         y_out(2)
         fetch_a(2)
-        fetch_far(0, whole)
-        w23s_d = deal(w23s, U8, "w23s_d")
-        w3w_d = deal(w3w, I32, "w3w_d")
-        for t in range(PACK): product(d_ps[t][:], w3w_d, w23s_d, 0, t, xb_w[:], xb_s[:])
-        fetch_b(2)
-        put(2)
         y_out(3)
         fetch_a(3)
+        fetch_far(0, whole)
+        fetch_b(2)
+        put(2)
         fetch_far(1, whole)
         z_row(0, whole)
         fetch_b(3)
@@ -262,13 +266,14 @@ def tile_picked_latesoftbfoldd_none_po_kernel(
         d_fetch(0)
         fetch_far(2, whole)
         z_row(1, whole)
-        d_out(1)
         d_tanh(1)
+        d_out(1)
+        d_out_v(3)
         z_row(2, whole)
         w2w_d = deal(w2w, I32, "w2w_d")
+        w2s_d = deal(w2s, U8, "w2s_d")
         fetch_far(3, cols(0))
         fetch_far(3, cols(1))
-        gate[0] = keep.tile([P, 2, S], F32, name="gate0")
         z_row(3, cols(0))
         z_row(3, cols(1))
         g0 = group(z_rows[:, :, cols(0)], HALF, "z0")
@@ -276,50 +281,43 @@ def tile_picked_latesoftbfoldd_none_po_kernel(
         c0 = z_codes(g0, "z0")
         c1 = z_codes(g1, "z1")
         z_products([c0, c1])
-        d_gate(0)
-        d_fetch(1)
-        d_gate(1)
+        gate[0] = keep.tile([P, 2, S], F32, name="gate0", tag="z0_g", align_bytes=64)
         d_out(2)
+        d_fetch(1)
         d_tanh(2)
         d_fetch(2)
-        d_out(3)
         d_tanh(3)
         d_fetch(3)
+        d_gate(0)
         gate[1] = keep.tile([P, 2, S], F32, name="gate1", tag="z1_w", align_bytes=64)
         h_out(0, whole)
+        d_gate(1)
         h_out(1, whole)
         h_out(2, whole)
-        d_gate(2)
         h_out(3, whole)
-        d_gate(3)
-        h_room(0, "h4_0")
-        h_room(1, "th3")
-        h_room(2, "d53")
+        d_gate(2)
+        h_room(0, 0)
+        h_room(1, 0)
         h_fetch(0, 0)
         h_fetch(1, 0)
         result(0, 0)
+        d_gate(3)
         h_fetch(2, 0)
         h_fetch(3, 0)
         result(1, 0)
         store_result(0)
+        h_room(0, 1)
         h_fetch(0, 1)
         h_fetch(1, 1)
-        result(0, 1)
+        o0 = group(res[0][:], parts[0].stop, "o0")
+        h_room(1, 1)
         h_fetch(2, 1)
         h_fetch(3, 1)
-        o0 = group(res[0][:], 256, "o0")
-        result(1, 1)
-        store_result(1)
         planes(o0, 0)
-        h_fetch(0, 2)
-        h_fetch(1, 2)
-        o1 = group(res[1][:], 128, "o1")
-        result(0, 2)
-        h_fetch(2, 2)
-        h_fetch(3, 2)
+        result(0, 1)
+        result_row(2, 1)
+        result_row(3, 1)
+        store_result(1)
+        o1 = group(res[1][:], S - parts[0].stop, "o1")
         planes(o1, 1)
-        result(1, 2)
-        store_result(2)
-        o2 = group(res[2][:], 128, "o2")
-        planes(o2, 2)
         store_scales()

@@ -58,10 +58,11 @@ def tile_picked_latesoftbfoldd_none_po_kernel(
                 )
 
         def deal(src, dtype, name):
+            run = 4 if dtype == I32 else 16
             tile = keep.tile([P, 512], dtype, name=name, align_bytes=64)
             nc.vector.tensor_copy(
-                tile[:].rearrange("p (t m) -> p m t", t=PACK),
-                src[:].rearrange("p (m t) -> p m t", t=PACK),
+                tile[:].rearrange("p (t c i) -> p c t i", t=PACK, i=run),
+                src[:].rearrange("p (c i t) -> p c t i", t=PACK, i=run),
             )
             return tile
 
@@ -99,9 +100,9 @@ def tile_picked_latesoftbfoldd_none_po_kernel(
             nc.vector.tensor_copy(tile[:], xs[:].indirect(lst[:]))
             return tile
 
-        def pick_words(lst, name, tag):
-            tile = keep.tile([P, S], I32, name=name, tag=tag, align_bytes=64)
-            nc.vector.tensor_copy(tile[:].bitcast(U32), xw[:].bitcast(U32).indirect(lst[:]))
+        def pick_words(lst, width, name, tag):
+            tile = keep.tile([P, width], I32, name=name, tag=tag, align_bytes=64)
+            nc.vector.tensor_copy(tile[:].bitcast(U32), xw[:].bitcast(U32).indirect(lst))
             return tile
 
         def product(bank, ww, ws, first, t, codes, scales):
@@ -114,23 +115,23 @@ def tile_picked_latesoftbfoldd_none_po_kernel(
         xa_s = pick_scales(offs_t, "xa_s")
         xb_s = pick_scales(two_t, "xb_s")
         w1w_d = deal(w1w, I32, "w1w_d")
-        xa_w = pick_words(offs_t, "xa_w", "xa_w")
+        xa_w = pick_words(offs_t[:], S, "xa_w", "xa_w")
         w1s_d = deal(w1s, U8, "w1s_d")
         y_ps = [psum.tile([P, S], F32, name="y_ps%d" % t, tag="yh%d" % t) for t in range(PACK)]
         for t in range(PACK):
             product(y_ps[t][:], w1w_d, w1s_d, 0, t, xa_w[:], xa_s[:])
-        xb_w = pick_words(two_t, "xb_w", "w1s")
+        xb_w = pick_words(two_t[:], S, "xb_w", "w1s")
 
-        ds = [keep.tile([P, 2 * S], F32, name="ds%d" % t) for t in range(PACK)]
+        ds = [keep.tile([P, 2 * S if t < PACK - 1 else S], F32, name="ds%d" % t) for t in range(PACK)]
         d_sb = [keep.tile([P, S + 16], F32, name="d_sb%d" % t) for t in range(PACK)]
-        for t in range(PACK):
+        for t in range(PACK - 1):
             nc.gpsimd.memset(ds[t][:, S:], 0.0)
         for t in range(PACK):
             nc.gpsimd.memset(d_sb[t][:, S:], 0.0)
         pa = [keep.tile([P, W], F32, name="pa%d" % t) for t in range(PACK)]
         pb = {}
         far = [keep.tile([P, S], F32, name="far%d" % t) for t in range(PACK)]
-        z_rows = keep.tile([P, PACK, S], BF16, name="z_rows")
+        z_rows = keep.tile([P, PACK, S], F32, name="z_rows")
         th = [keep.tile([P, S], F32, name="th%d" % t, tag="th%d" % t) for t in range(PACK)]
         d5 = [keep.tile([P, S], F32, name="d5%d" % t, tag="d5%d" % t) for t in range(PACK)]
         gate = {}
@@ -143,6 +144,12 @@ def tile_picked_latesoftbfoldd_none_po_kernel(
 
         def y_out(t):
             nc.scalar.activation(ds[t][:, :S], y_ps[t][:], COPY, scale=gain[:, t : t + 1])
+
+        def y_out_half(t, a):
+            nc.scalar.activation(ds[t][:, cols(a)], y_ps[t, a][:], COPY, scale=gain[:, t : t + 1])
+
+        def d_gate_g(t):
+            nc.gpsimd.tensor_tensor(gate[t // 2][:, t % 2, :], th[t][:], d5[t][:], MULT)
 
         def fetch_a(t):
             nc.scalar.activation(pa[t][:], ds[t][:].indirect(n1_t[:]), COPY)
@@ -178,23 +185,22 @@ def tile_picked_latesoftbfoldd_none_po_kernel(
         def group(rows, width, name):
             grouped = keep.tile([P, width, PACK], BF16, name=name + "_g", tag=name + "_g", align_bytes=64)
             nc.vector.tensor_copy(
-                grouped[:].rearrange("p (c i) t -> p c t i", i=4),
-                rows.rearrange("p t (c i) -> p c t i", i=4),
+                grouped[:].rearrange("p (c i) t -> p c t i", i=2),
+                rows.rearrange("p t (c i) -> p c t i", i=2),
             )
             return grouped
 
-        def z_codes(grouped, name):
-            z_w = keep.tile([P, HALF], I32, name=name + "_w", tag=name + "_w", align_bytes=64)
-            z_s = keep.tile([P, HALF], U8, name=name + "_s", align_bytes=64)
-            nc.vector.quantize_mx(
-                out=z_w[:].bitcast(FP8X4), scales=z_s[:], in_=grouped[:].rearrange("p j t -> p (j t)")
-            )
-            return z_w, z_s
+        z_w = keep.tile([P, S], I32, name="z_w", tag="z_w", align_bytes=64)
+        z_s = keep.tile([P, S], U8, name="z_s", align_bytes=64)
 
-        def z_products(codes):
+        def z_codes(grouped, a):
+            nc.vector.quantize_mx(
+                out=z_w[:, cols(a)].bitcast(FP8X4), scales=z_s[:, cols(a)], in_=grouped[:].rearrange("p j t -> p (j t)")
+            )
+
+        def z_products():
             for t in range(PACK):
-                for a in range(2):
-                    product(h_ps[t][:, cols(a)], w2w_d, w2s_d, 0, t, codes[a][0][:], codes[a][1][:])
+                product(h_ps[t][:], w2w_d, w2s_d, 0, t, z_w[:], z_s[:])
 
         def h_out(t, c):
             nc.vector.tensor_copy(h_sb[t][:, c], h_ps[t][:, c])
@@ -278,30 +284,30 @@ def tile_picked_latesoftbfoldd_none_po_kernel(
         z_row(3, cols(1))
         g0 = group(z_rows[:, :, cols(0)], HALF, "z0")
         g1 = group(z_rows[:, :, cols(1)], HALF, "z1")
-        c0 = z_codes(g0, "z0")
-        c1 = z_codes(g1, "z1")
-        z_products([c0, c1])
+        z_codes(g0, 0)
+        z_codes(g1, 1)
+        z_products()
         gate[0] = keep.tile([P, 2, S], F32, name="gate0", tag="z0_g", align_bytes=64)
-        d_out(2)
+        gate[1] = keep.tile([P, 2, S], F32, name="gate1", tag="z1_g", align_bytes=64)
         d_fetch(1)
         d_tanh(2)
-        d_fetch(2)
         d_tanh(3)
+        d_out_v(2)
         d_fetch(3)
-        d_gate(0)
-        gate[1] = keep.tile([P, 2, S], F32, name="gate1", tag="z1_w", align_bytes=64)
+        d_fetch(2)
+        d_gate_g(0)
+        d_gate_g(1)
+        d_gate_g(3)
         h_out(0, whole)
-        d_gate(1)
         h_out(1, whole)
         h_out(2, whole)
         h_out(3, whole)
-        d_gate(2)
         h_room(0, 0)
         h_room(1, 0)
         h_fetch(0, 0)
         h_fetch(1, 0)
         result(0, 0)
-        d_gate(3)
+        d_gate(2)
         h_fetch(2, 0)
         h_fetch(3, 0)
         result(1, 0)

from contextlib import ExitStack

import concourse.mybir as mybir

K, T, S, N, H, W = 512, 2048, 512, 512, 512, 256
FLOPS = 3 * 2 * 512 * 512 * 512

F32 = mybir.dt.float32
BF16 = mybir.dt.bfloat16
I32 = mybir.dt.int32
U32 = mybir.dt.uint32
U16 = mybir.dt.uint16
U8 = mybir.dt.uint8
FP8X4 = mybir.dt.float8_e4m3fn_x4
MULT = mybir.AluOpType.mult
ADD = mybir.AluOpType.add
SUB = mybir.AluOpType.subtract
COPY = mybir.ActivationFunctionType.Copy
TANH = mybir.ActivationFunctionType.Tanh

P = 128
PACK = 4
HALF = S // 2


def tile_picked_latesoftbfoldd_none_po_kernel(
    tc, x_words, x_scales, w1_words, w1_scales, gn, w2_words, w2_scales, w3_words, w3_scales,
    offs, n1, n2, n3, two, n4, n5, out_0, out_1, out_2,
):
    nc = tc.nc
    with ExitStack() as ctx:
        lists = ctx.enter_context(tc.tile_pool(name="lists", bufs=1))
        keep = ctx.enter_context(tc.tile_pool(name="keep", bufs=1))
        psum = ctx.enter_context(tc.psum_pool(name="psum", bufs=1))

        def load_list(src, name):
            tile = lists.tile(list(src.shape), U16, name=name)
            nc.sync.dma_start(tile[:], src)
            return tile

        def load_words(src, cols, name, queue):
            tile = keep.tile([P, cols], I32, name=name, align_bytes=64)
            queue.dma_start(tile[:], src[0].rearrange("p c r -> p (c r)").bitcast(I32))
            return tile

        def load_scale_rows(tile, src, first, queue):
            for q in range(4):
                queue.dma_start(
                    tile[32 * q + first : 32 * q + first + 4, :].bitcast(I32),
                    src[0, 4 * q : 4 * q + 4, :].bitcast(I32),
                )

        def load_scale_rows_repeated(tile, src, queues):
            for q in range(4):
                queues[q].dma_start(
                    tile[32 * q : 32 * q + 32, :].bitcast(I32),
                    src[0, 4 * q : 4 * q + 4, :].bitcast(I32).partition_broadcast(8),
                )

        def deal(src, dtype, name):
            run = 4 if dtype == I32 else 16
            tile = keep.tile([P, 512], dtype, name=name, align_bytes=64)
            nc.vector.tensor_copy(
                tile[:].rearrange("p (t c i) -> p c t i", t=PACK, i=run),
                src[:].rearrange("p (c i t) -> p c t i", t=PACK, i=run),
            )
            return tile

        def half_list(tile, a):
            return tile[:, a * (HALF // 16) : (a + 1) * (HALF // 16)]

        def cols(a):
            return slice(a * HALF, (a + 1) * HALF)

        xs = keep.tile([P, T], U8, name="xs", align_bytes=64)
        w1s = keep.tile([P, H], U8, name="w1s", tag="w1s", align_bytes=64)
        w2s = keep.tile([P, N], U8, name="w2s", align_bytes=64)
        w3s = keep.tile([P, N], U8, name="w3s", tag="w3s", align_bytes=64)

        offs_t = load_list(offs, "offs_t")
        load_scale_rows_repeated(xs, x_scales, [nc.scalar, nc.scalar, nc.scalar, nc.sync])
        two_t = load_list(two, "two_t")
        w1w = load_words(w1_words, H, "w1w", nc.sync)
        xw = load_words(x_words, T, "xw", nc.scalar)
        load_scale_rows_repeated(w1s, w1_scales, [nc.sync] * 4)
        gain = keep.tile([P, PACK], F32, name="gain")
        nc.scalar.dma_start(gain[:], gn.rearrange("(p t) o -> p (t o)", t=PACK))
        n1_t = load_list(n1, "n1_t")
        n2_t = load_list(n2, "n2_t")
        w3w = load_words(w3_words, N, "w3w", nc.scalar)
        load_scale_rows_repeated(w3s, w3_scales, [nc.scalar, nc.scalar, nc.scalar, nc.sync])
        n3_t = load_list(n3, "n3_t")
        n5_t = load_list(n5, "n5_t")
        load_scale_rows_repeated(w2s, w2_scales, [nc.sync] * 4)
        w2w = load_words(w2_words, N, "w2w", nc.sync)
        n4_t = load_list(n4, "n4_t")

        def pick_scales(lst, name):
            tile = keep.tile([P, S], U8, name=name, align_bytes=64)
            nc.vector.tensor_copy(tile[:], xs[:].indirect(lst[:]))
            return tile

        def pick_words(lst, width, name, tag):
            tile = keep.tile([P, width], I32, name=name, tag=tag, align_bytes=64)
            nc.vector.tensor_copy(tile[:].bitcast(U32), xw[:].bitcast(U32).indirect(lst))
            return tile

        def product(bank, ww, ws, first, t, codes, scales):
            m = slice(P * t, P * (t + 1))
            nc.tensor.matmul_mx(
                out=bank, lhsT=ww[:, m].bitcast(FP8X4), lhsT_scale=ws[first:P, m],
                rhs=codes.bitcast(FP8X4), rhs_scale=scales, start=True, stop=True,
            )

        xa_s = pick_scales(offs_t, "xa_s")
        xb_s = pick_scales(two_t, "xb_s")
        w1w_d = deal(w1w, I32, "w1w_d")
        xa_w = pick_words(offs_t[:], S, "xa_w", "xa_w")
        w1s_d = deal(w1s, U8, "w1s_d")
        y_ps = [psum.tile([P, S], F32, name="y_ps%d" % t, tag="yh%d" % t) for t in range(PACK)]
        for t in range(PACK):
            product(y_ps[t][:], w1w_d, w1s_d, 0, t, xa_w[:], xa_s[:])
        xb_w = pick_words(two_t[:], S, "xb_w", "w1s")

        ds = [keep.tile([P, 2 * S if t < PACK - 1 else S], F32, name="ds%d" % t) for t in range(PACK)]
        d_sb = [keep.tile([P, S + 16], F32, name="d_sb%d" % t) for t in range(PACK)]
        for t in range(PACK - 1):
            nc.gpsimd.memset(ds[t][:, S:], 0.0)
        for t in range(PACK):
            nc.gpsimd.memset(d_sb[t][:, S:], 0.0)
        pa = [keep.tile([P, W], F32, name="pa%d" % t) for t in range(PACK)]
        pb = {}
        far = [keep.tile([P, S], F32, name="far%d" % t) for t in range(PACK)]
        z_rows = keep.tile([P, PACK, S], F32, name="z_rows")
        th = [keep.tile([P, S], F32, name="th%d" % t, tag="th%d" % t) for t in range(PACK)]
        d5 = [keep.tile([P, S], F32, name="d5%d" % t, tag="d5%d" % t) for t in range(PACK)]
        gate = {}
        h_sb = [keep.tile([P, S], F32, name="h_sb%d" % t) for t in range(PACK)]
        d_ps = [psum.tile([P, S], F32, name="d_ps%d" % t, tag="d%d" % t) for t in range(PACK)]
        h_ps = [psum.tile([P, S], F32, name="h_ps%d" % t, tag="yh%d" % t) for t in range(PACK)]

        def part_list(tile, c):
            return tile[:, c.start // 16 : c.stop // 16]

        def y_out(t):
            nc.scalar.activation(ds[t][:, :S], y_ps[t][:], COPY, scale=gain[:, t : t + 1])

        def y_out_half(t, a):
            nc.scalar.activation(ds[t][:, cols(a)], y_ps[t, a][:], COPY, scale=gain[:, t : t + 1])

        def d_gate_g(t):
            nc.gpsimd.tensor_tensor(gate[t // 2][:, t % 2, :], th[t][:], d5[t][:], MULT)

        def fetch_a(t):
            nc.scalar.activation(pa[t][:], ds[t][:].indirect(n1_t[:]), COPY)

        def fetch_b(t):
            pb[t] = keep.tile([P, W], F32, name="pb%d" % t, tag="pb%d" % t)
            nc.vector.tensor_scalar(pb[t][:], ds[t][:].indirect(n2_t[:]), -0.5, 0.0, MULT, ADD)

        def put(t):
            nc.vector.tensor_tensor(ds[t][:].indirect(n2_t[:]), pa[t][:], pb[t][:], ADD)

        def fetch_far(t, c):
            nc.scalar.activation(far[t][:, c], ds[t][:].indirect(part_list(n3_t, c)), COPY)

        def z_row(t, c):
            nc.vector.scalar_tensor_tensor(z_rows[:, t, c], far[t][:, c], -0.5, ds[t][:, c], MULT, ADD)

        def d_out(t):
            nc.scalar.activation(d_sb[t][:, :S], d_ps[t][:], COPY)

        def d_out_v(t):
            nc.vector.tensor_copy(d_sb[t][:, :S], d_ps[t][:])

        def d_tanh(t):
            nc.scalar.activation(th[t][:], d_ps[t][:], TANH)

        def d_fetch(t):
            nc.scalar.activation(d5[t][:], d_sb[t][:].indirect(n5_t[:]), COPY)

        def d_gate(t):
            nc.vector.tensor_tensor(gate[t // 2][:, t % 2, :], th[t][:], d5[t][:], MULT)

        def group(rows, width, name):
            grouped = keep.tile([P, width, PACK], BF16, name=name + "_g", tag=name + "_g", align_bytes=64)
            nc.vector.tensor_copy(
                grouped[:].rearrange("p (c i) t -> p c t i", i=2),
                rows.rearrange("p t (c i) -> p c t i", i=2),
            )
            return grouped

        z_w = keep.tile([P, S], I32, name="z_w", tag="z_w", align_bytes=64)
        z_s = keep.tile([P, S], U8, name="z_s", align_bytes=64)

        def z_codes(grouped, a):
            nc.vector.quantize_mx(
                out=z_w[:, cols(a)].bitcast(FP8X4), scales=z_s[:, cols(a)], in_=grouped[:].rearrange("p j t -> p (j t)")
            )

        def z_products():
            for t in range(PACK):
                product(h_ps[t][:], w2w_d, w2s_d, 0, t, z_w[:], z_s[:])

        def h_out(t, c):
            nc.vector.tensor_copy(h_sb[t][:, c], h_ps[t][:, c])

        def h_out_s(t, c):
            nc.scalar.activation(h_sb[t][:, c], h_ps[t][:, c], COPY)

        out_rows = out_0.rearrange("(p t) j -> p t j", t=PACK)
        out_words = out_1[0].rearrange("p c r -> p (c r)").bitcast(I32)
        o_s = keep.tile([P, S], U8, name="o_s", align_bytes=64)
        parts = [slice(0, HALF), slice(HALF, S)]
        h4 = {}
        res = [keep.tile([P, PACK, c.stop - c.start], F32, name="res_%d" % c.start) for c in parts]

        def h_room(u, a):
            h4[u, a] = keep.tile([P, 2, parts[a].stop - parts[a].start], F32, name="h4_%d_%d" % (u, a), tag="h4_%d" % u)

        def h_fetch(t, a):
            nc.scalar.activation(h4[t // 2, a][:, t % 2, :], h_sb[t][:].indirect(part_list(n4_t, parts[a])), COPY)

        def result(u, a):
            ts = slice(2 * u, 2 * u + 2)
            nc.vector.tensor_tensor(res[a][:, ts, :], h4[u, a][:], gate[u][:, :, parts[a]], SUB)

        def result_row(t, a):
            nc.vector.tensor_tensor(res[a][:, t, :], h4[t // 2, a][:, t % 2, :], gate[t // 2][:, t % 2, parts[a]], SUB)

        def store_result(a):
            nc.sync.dma_start(out_rows[:, :, parts[a]], res[a][:])

        def planes(grouped, a):
            c = parts[a]
            o_w = keep.tile([P, c.stop - c.start], I32, name="o_w%d" % a, align_bytes=64)
            nc.vector.quantize_mx(
                out=o_w[:].bitcast(FP8X4), scales=o_s[:, c], in_=grouped[:].rearrange("p j t -> p (j t)")
            )
            nc.sync.dma_start(out_words[:, c], o_w[:])

        def store_scales():
            for q in range(4):
                queue = nc.sync if q % 2 == 0 else nc.scalar
                queue.dma_start(out_2[0, 4 * q : 4 * q + 4, :].bitcast(I32), o_s[32 * q : 32 * q + 4, :].bitcast(I32))

        whole = slice(0, S)
        y_out(0)
        fetch_a(0)
        fetch_b(0)
        put(0)
        w3s_d = deal(w3s, U8, "w3s_d")
        w3w_d = deal(w3w, I32, "w3w_d")
        for t in range(PACK): product(d_ps[t][:], w3w_d, w3s_d, 0, t, xb_w[:], xb_s[:])
        y_out(1)
        fetch_a(1)
        fetch_b(1)
        put(1)
        y_out(2)
        fetch_a(2)
        y_out(3)
        fetch_a(3)
        fetch_far(0, whole)
        fetch_b(2)
        put(2)
        fetch_far(1, whole)
        z_row(0, whole)
        fetch_b(3)
        put(3)
        d_out(0)
        d_tanh(0)
        d_fetch(0)
        fetch_far(2, whole)
        z_row(1, whole)
        d_tanh(1)
        d_out(1)
        d_out_v(3)
        z_row(2, whole)
        w2w_d = deal(w2w, I32, "w2w_d")
        w2s_d = deal(w2s, U8, "w2s_d")
        fetch_far(3, cols(0))
        fetch_far(3, cols(1))
        z_row(3, cols(0))
        z_row(3, cols(1))
        g0 = group(z_rows[:, :, cols(0)], HALF, "z0")
        g1 = group(z_rows[:, :, cols(1)], HALF, "z1")
        z_codes(g0, 0)
        z_codes(g1, 1)
        z_products()
        gate[0] = keep.tile([P, 2, S], F32, name="gate0", tag="z0_g", align_bytes=64)
        gate[1] = keep.tile([P, 2, S], F32, name="gate1", tag="z1_g", align_bytes=64)
        d_fetch(1)
        d_tanh(2)
        d_tanh(3)
        d_out_v(2)
        d_fetch(3)
        d_fetch(2)
        d_gate_g(0)
        d_gate_g(1)
        d_gate_g(3)
        h_out(0, whole)
        h_out(1, whole)
        h_out(2, whole)
        h_out(3, whole)
        h_room(0, 0)
        h_room(1, 0)
        h_fetch(0, 0)
        h_fetch(1, 0)
        result(0, 0)
        d_gate(2)
        h_fetch(2, 0)
        h_fetch(3, 0)
        result(1, 0)
        store_result(0)
        h_room(0, 1)
        h_fetch(0, 1)
        h_fetch(1, 1)
        o0 = group(res[0][:], parts[0].stop, "o0")
        h_room(1, 1)
        h_fetch(2, 1)
        h_fetch(3, 1)
        planes(o0, 0)
        result(0, 1)
        result_row(2, 1)
        result_row(3, 1)
        store_result(1)
        o1 = group(res[1][:], S - parts[0].stop, "o1")
        planes(o1, 1)
        store_scales()
